import numpy as np
import ml_dtypes


def mxq(x, axis, fmt="e4m3"):
    dtype, down = {"e4m3": (ml_dtypes.float8_e4m3fn, 7), "e5m2": (ml_dtypes.float8_e5m2, 14)}[fmt]
    v = np.moveaxis(np.asarray(x, np.float32).astype(ml_dtypes.bfloat16).astype(np.float64), axis, -1)
    blocks = v.reshape(v.shape[:-1] + (-1, 32))
    amax = np.abs(blocks).max(-1, keepdims=True)
    byte = np.maximum(np.where(amax > 0, np.frexp(amax)[1] - 1 + 127, 0) - down, 1)
    scale = np.exp2(byte - 127.0)
    codes = (blocks / scale).astype(np.float32).astype(dtype).astype(np.float64)
    return np.moveaxis((codes * scale).reshape(v.shape), -1, axis)


WIDE = False


def mx_kscale(k):
    if not WIDE:
        return np.ones(k)
    levels = np.array([10, -10, 5, -5, 0])
    if k % 512:
        return np.exp2(np.random.permutation(np.resize(levels, k // 32))).repeat(32)
    a = np.empty((k // 512, 16))
    for p in range(k // 512):
        a[p, :8] = np.random.permutation(np.resize(levels, 8))
        for g in range(8):
            far = levels[np.abs(levels - a[p, g]) >= 10]
            a[p, g + 8] = far[np.random.randint(len(far))]
    return np.exp2(a.ravel()).repeat(32)


def f64(x):
    return np.asarray(x).astype(np.float64)


def striped(idx):
    return np.tile(idx.reshape(-1, 16).T, (8, 1)).astype(np.uint16)


def unstriped(offs):
    return offs[:16].T.reshape(-1).astype(np.int64)


def striped8(idx):
    return np.concatenate([x.reshape(-1, 16).T for x in idx]).astype(np.uint16)


def runs(offs, k):
    lists = np.stack([offs[16 * r : 16 * r + 16].T.reshape(-1) for r in range(8)]).astype(np.int64)
    return lists[np.arange(k) % 512 // 64]


def pack_weight(w):
    k, n = w.shape
    w = f64(np.asarray(w, np.float32).astype(ml_dtypes.bfloat16)).reshape(k // 32, 32, n)
    amax = np.abs(w).max(1)
    byte = np.clip(np.where(amax > 0, np.frexp(amax)[1] - 1 + 127 - 7, 1), 1, 254)
    scaled = (w * np.exp2(127.0 - byte)[:, None, :]).reshape(k, n).astype(np.float32)
    words = np.ascontiguousarray(scaled.reshape(k // 512, 128, 4, n).transpose(0, 1, 3, 2)).astype(ml_dtypes.float8_e4m3fn).view(np.uint8)
    return words, np.ascontiguousarray(byte.astype(np.uint8).reshape(k // 512, 16, n))


def unpack_weight(words, scales):
    g, p, n, _ = words.shape
    vals = np.ascontiguousarray(words).view(ml_dtypes.float8_e4m3fn).astype(np.float64) * np.repeat(np.exp2(scales.astype(np.float64) - 127.0), 8, axis=1)[..., None]
    return vals.transpose(0, 1, 3, 2).reshape(g * 512, n)

def planes(y):
    n, m = y.shape
    v = y.astype(np.float32).astype(ml_dtypes.bfloat16).astype(np.float64).reshape(n // 32, 32, m)
    top = np.abs(v).max(1)
    byte = np.clip(np.where(top > 0, np.frexp(top)[1] - 1 + 127 - 7, 1), 1, 254)
    codes = (v * np.exp2(127.0 - byte)[:, None, :]).reshape(n, m).astype(np.float32).astype(ml_dtypes.float8_e4m3fn).view(np.uint8)
    words = codes.reshape(n // 512, 128, 4, m).transpose(0, 1, 3, 2)
    return np.ascontiguousarray(words), np.ascontiguousarray(byte.astype(np.uint8).reshape(n // 512, 16, m))


K, T, S, N, H = 512, 2048, 512, 512, 512


def setup_inputs():
    n = np.random.standard_normal
    s = mx_kscale(K)[:, None]
    u = mx_kscale(H)
    packed_xT = pack_weight(n((K, T)) * s)
    packed_w1 = pack_weight(n((K, H)) / np.sqrt(K) / s)
    packed_w2 = pack_weight(n((H, N)) / np.sqrt(H) / u[:, None])
    packed_w3 = pack_weight(n((H, N)) / np.sqrt(H) / u[:, None])
    return {
        "x_words": packed_xT[0],
        "x_scales": packed_xT[1],
        "w1_words": packed_w1[0],
        "w1_scales": packed_w1[1],
        "gn": (np.random.uniform(0.5, 1.5, (H, 1)) * u[:, None]).astype(np.float32),
        "w2_words": packed_w2[0],
        "w2_scales": packed_w2[1],
        "gm": (np.random.uniform(0.5, 1.5, (H, 1)) * u[:, None]).astype(np.float32),
        "w3_words": packed_w3[0],
        "w3_scales": packed_w3[1],
        "offs": striped(np.random.permutation(T)[:S]),
        "n1": striped8(np.stack([np.random.permutation(S) for _ in range(8)])),
        "n2": striped8(np.stack([np.random.permutation(S) for _ in range(8)])),
        "n3": striped8(np.stack([np.random.permutation(S) for _ in range(8)])),
        "n4": striped8(np.stack([np.random.permutation(S) for _ in range(8)])),
        "n5": striped8(np.stack([np.random.permutation(S) for _ in range(8)])),
    }


def reference(x_words, x_scales, w1_words, w1_scales, gn, w2_words, w2_scales, gm, w3_words, w3_scales, offs, n1, n2, n3, n4, n5):
    xq = unpack_weight(x_words, x_scales)[:, unstriped(offs)]
    y = unpack_weight(w1_words, w1_scales).T @ xq
    z = f64(gn) * (np.maximum(y, y[np.arange(H)[:, None], runs(n1, H)]))
    a = unpack_weight(w2_words, w2_scales).T @ mxq(z, 0, "e4m3")
    ex = np.exp(0.5 * y)
    z2 = f64(gm) * ((2.0 * ex) / (ex + ex[np.arange(H)[:, None], runs(n2, H)] + ex[np.arange(H)[:, None], runs(n3, H)]))
    b = unpack_weight(w3_words, w3_scales).T @ mxq(z2, 0, "e4m3")
    out_0 = a[np.arange(N)[:, None], runs(n4, N)] - (np.tanh(b) * (b[np.arange(N)[:, None], runs(n5, N)]))
    return (out_0,) + planes(out_0)

@@ -1,0 +1,216 @@
+from contextlib import ExitStack
+
+import concourse.mybir as mybir
+from concourse.masks import make_identity
+
+F32 = mybir.dt.float32
+BF16 = mybir.dt.bfloat16
+I32 = mybir.dt.int32
+U32 = mybir.dt.uint32
+U16 = mybir.dt.uint16
+U8 = mybir.dt.uint8
+FP8X4 = mybir.dt.float8_e4m3fn_x4
+ALU = mybir.AluOpType
+ACT = mybir.ActivationFunctionType
+
+P = 128
+PACK = 4
+T = 2048
+S = 512
+HALF = S // 2
+FLOPS = 3 * 2 * 512 * 512 * 512
+
+
+def tile_picked_forksoftbbigshare_none_po_kernel(
+    tc, x_words, x_scales, w1_words, w1_scales, gn, w2_words, w2_scales, gm, w3_words, w3_scales,
+    offs, n1, n2, n3, n4, n5, out_0, out_1, out_2,
+):
+    nc = tc.nc
+    with ExitStack() as ctx:
+        sb = ctx.enter_context(tc.tile_pool(name="sb", bufs=1))
+        ps = ctx.enter_context(tc.psum_pool(name="ps", bufs=1))
+
+        def load_list(src, name):
+            tile = sb.tile([P, S // 16], U16, name=name)
+            nc.sync.dma_start(tile[:], src)
+            return tile
+
+        def load_words(src, name, cols, queue, tag):
+            tile = sb.tile([P, cols], U32, name=name, tag=tag, align_bytes=64)
+            queue.dma_start(tile[:].bitcast(I32), src[0].rearrange("p c r -> p (c r)").bitcast(I32))
+            return tile
+
+        def load_scales(tile, src, row, queues):
+            for q, queue in enumerate(queues):
+                queue.dma_start(
+                    tile[32 * q + row : 32 * q + row + 4, :].bitcast(I32),
+                    src[0, 4 * q : 4 * q + 4, :].bitcast(I32),
+                )
+
+        def deal(src, name, dtype, view):
+            tile = sb.tile([P, S], dtype, name=name, align_bytes=64)
+            nc.vector.tensor_copy(
+                tile[:].bitcast(view).rearrange("p (t m) -> p t m", t=PACK),
+                src[:].bitcast(view).rearrange("p (m t) -> p t m", t=PACK),
+            )
+            return tile
+
+        def interleave(dst, src, copy=nc.vector.tensor_copy):
+            copy(
+                dst.rearrange("p (c i t) -> p c t i", i=4, t=PACK),
+                src.rearrange("p t (c i) -> p c t i", i=4),
+            )
+
+        def product(bank, words, scales, row, t, codes, code_scales):
+            cols = slice(t * P, (t + 1) * P)
+            nc.tensor.matmul_mx(
+                out=bank[:], lhsT=words[:, cols].bitcast(FP8X4), lhsT_scale=scales[row:P, cols],
+                rhs=codes[:].bitcast(FP8X4), rhs_scale=code_scales[:], start=True, stop=True,
+            )
+
+        xs = sb.tile([P, T], U8, name="xs", tag="xs", align_bytes=64)
+        w1s = sb.tile([P, S], U8, name="w1s", align_bytes=64)
+        nc.vector.memset(xs[:].bitcast(I32), 0)
+        nc.gpsimd.memset(w1s[:].bitcast(I32), 0)
+
+        offs_t = load_list(offs, "offs_t")
+        n1_t = load_list(n1, "n1_t")
+        n2_t = load_list(n2, "n2_t")
+        n3_t = load_list(n3, "n3_t")
+        n4_t = load_list(n4, "n4_t")
+        n5_t = load_list(n5, "n5_t")
+        w1w = load_words(w1_words, "w1w", S, nc.sync, "w1w")
+        xw = load_words(x_words, "xw", T, nc.sync, "xw")
+        load_scales(xs, x_scales, 0, [nc.sync] * 4)
+        load_scales(w1s, w1_scales, 0, [nc.gpsimd, nc.sync, nc.sync, nc.sync])
+        gn_t = sb.tile([P, PACK], F32, name="gn_t")
+        nc.gpsimd.dma_start(gn_t[:], gn.rearrange("(p t) o -> p (t o)", t=PACK))
+        gm_t = sb.tile([P, PACK], F32, name="gm_t")
+        nc.gpsimd.dma_start(gm_t[:], gm.rearrange("(p t) o -> p (t o)", t=PACK))
+
+        ident = sb.tile([P, P], F32, name="ident")
+        make_identity(nc, ident[:])
+
+        ywin = [sb.tile([P, 2 * S], F32, name=f"ywin{t}") for t in range(PACK)]
+        for t in range(PACK):
+            nc.vector.memset(ywin[t][:, S:], 0.0)
+
+        w1d = deal(w1w, "w1d", U32, I32)
+        xgs = sb.tile([P, S], U8, name="xgs", align_bytes=64)
+        nc.vector.tensor_copy(xgs[:], xs[:].indirect(offs_t[:]))
+        w1sd = deal(w1s, "w1sd", U8, U8)
+        xg = sb.tile([P, S], U32, name="xg", align_bytes=64)
+        nc.vector.tensor_copy(xg[:], xw[:].indirect(offs_t[:]))
+
+        w2w = load_words(w2_words, "w2w", S, nc.sync, "xw")
+        w3w = load_words(w3_words, "w3w", S, nc.sync, "w1w")
+        w23s = sb.tile([P, S], U8, name="w23s", tag="xs", align_bytes=64)
+        nc.gpsimd.memset(w23s[:].bitcast(I32), 0)
+        load_scales(w23s, w2_scales, 0, [nc.sync] * 4)
+        load_scales(w23s, w3_scales, 4, [nc.sync] * 4)
+
+        ybank = [ps.tile([P, S], F32, name=f"ybank{t}", tag=f"A{t}") for t in range(PACK)]
+        for t in range(PACK):
+            product(ybank[t], w1d, w1sd, 0, t, xg, xgs)
+        for t in range(PACK):
+            nc.scalar.copy(ywin[t][:, :S], ybank[t][:])
+
+        ex = sb.tile([P, PACK, S], F32, name="ex")
+        e2 = sb.tile([P, PACK, S], F32, name="e2")
+        e3 = sb.tile([P, PACK, S], F32, name="e3")
+        dbank = [ps.tile([P, PACK, P], F32, name=f"dbank{t}", tag=f"B{t}") for t in range(PACK)]
+        for t in range(PACK):
+            nc.scalar.activation(ex[:, t, :], ywin[t][:, :S], ACT.Exp, scale=0.5)
+            nc.scalar.activation(e2[:, t, :], ywin[t][:].indirect(n2_t[:]), ACT.Exp, scale=0.5)
+            nc.scalar.activation(e3[:, t, :], ywin[t][:].indirect(n3_t[:]), ACT.Exp, scale=0.5)
+            for j in range(PACK):
+                for i, term in enumerate((ex, e2, e3)):
+                    nc.tensor.matmul(
+                        dbank[t][:, j, :], lhsT=term[:, t, j * P : (j + 1) * P], rhs=ident[:],
+                        is_transpose=True, start=(i == 0), stop=(i == 2),
+                    )
+
+        awin = [sb.tile([P, 2 * S], F32, name=f"awin{t}") for t in range(PACK)]
+        big = sb.tile([P, PACK, S], F32, name="big")
+        zb = sb.tile([P, PACK, S], BF16, name="zb")
+        for t in range(PACK + 1):
+            if t < PACK:
+                nc.vector.tensor_copy(awin[t][:, S:], ywin[t][:].indirect(n1_t[:]))
+            if t > 0:
+                nc.vector.tensor_tensor(big[:, t - 1, :], awin[t - 1][:, S:], ybank[t - 1][:], ALU.max)
+        for t in range(PACK):
+            nc.vector.tensor_scalar(zb[:, t, :], big[:, t, :], gn_t[:, t : t + 1], None, ALU.mult)
+        w2d = deal(w2w, "w2d", U32, I32)
+        zi = sb.tile([P, PACK * S], BF16, name="zi", align_bytes=64)
+        interleave(zi[:], zb[:])
+        w23sd = deal(w23s, "w23sd", U8, U8)
+        zq = sb.tile([P, S], U32, name="zq", align_bytes=64)
+        zs = sb.tile([P, S], U8, name="zs", align_bytes=64)
+        nc.vector.quantize_mx(out=zq[:].bitcast(FP8X4), scales=zs[:], in_=zi[:])
+        w3d = deal(w3w, "w3d", U32, I32)
+        gm2 = sb.tile([P, PACK], F32, name="gm2")
+        nc.vector.tensor_scalar(gm2[:], gm_t[:], 2.0, None, ALU.mult)
+
+        abank = [ps.tile([P, S], F32, name=f"abank{t}", tag=f"A{t}") for t in range(PACK)]
+        for t in range(PACK):
+            product(abank[t], w2d, w23sd, 0, t, zq, zs)
+
+        root = sb.tile([P, PACK, S], F32, name="root")
+        inv = sb.tile([P, PACK, S], F32, name="inv")
+        z2b = sb.tile([P, PACK, S], BF16, name="z2b")
+        rbank = []
+        for t in range(PACK):
+            nc.scalar.activation(root[:, t, :], dbank[t][:].rearrange("p j m -> p (j m)"), ACT.Abs_reciprocal_sqrt)
+            nc.scalar.activation(inv[:, t, :], root[:, t, :], ACT.Square)
+            bank = ps.tile([P, PACK, P], F32, name=f"rbank{t}", tag=f"B{t}")
+            for j in range(PACK):
+                nc.tensor.transpose(bank[:, j, :], inv[:, t, j * P : (j + 1) * P], ident[:])
+            rbank.append(bank)
+        for t in range(PACK):
+            nc.vector.scalar_tensor_tensor(
+                z2b[:, t, :], ex[:, t, :], gm2[:, t : t + 1], rbank[t][:].rearrange("p j m -> p (j m)"), ALU.mult, ALU.mult
+            )
+        z2i = sb.tile([P, PACK * S], BF16, name="z2i", align_bytes=64)
+        interleave(z2i[:], z2b[:])
+        z2q = sb.tile([P, S], U32, name="z2q", align_bytes=64)
+        z2s = sb.tile([P, S], U8, name="z2s", align_bytes=64)
+        nc.vector.quantize_mx(out=z2q[:].bitcast(FP8X4), scales=z2s[:], in_=z2i[:])
+        bbank = [ps.tile([P, S], F32, name=f"bbank{t}", tag=f"B{t}") for t in range(PACK)]
+        for t in range(PACK):
+            product(bbank[t], w3d, w23sd, 4, t, z2q, z2s)
+
+        ga = sb.tile([P, PACK, S], F32, name="ga")
+        for t in range(PACK + 1):
+            if t < PACK:
+                nc.vector.tensor_copy(awin[t][:, :S], abank[t][:])
+            if t > 0:
+                nc.vector.tensor_copy(ga[:, t - 1, :], awin[t - 1][:].indirect(n4_t[:]))
+
+        bwin = [sb.tile([P, S], F32, name=f"bwin{t}") for t in range(PACK)]
+        th = sb.tile([P, PACK, S], F32, name="th")
+        for t in range(PACK):
+            nc.scalar.copy(bwin[t][:], bbank[t][:])
+            nc.scalar.activation(th[:, t, :], bbank[t][:], ACT.Tanh)
+
+        prod = sb.tile([P, PACK, S], F32, name="prod")
+        res = sb.tile([P, PACK, S], F32, name="res")
+        oi = sb.tile([P, PACK * S], BF16, name="oi", align_bytes=64)
+        oq = sb.tile([P, S], U32, name="oq", align_bytes=64)
+        osc = sb.tile([P, S], U8, name="osc", align_bytes=64)
+        out_rows = out_0.rearrange("(p t) c -> p t c", t=PACK)
+        out_words = out_1[0].rearrange("p c r -> p (c r)").bitcast(I32)
+        for h in range(2):
+            cols = slice(h * HALF, (h + 1) * HALF)
+            lcols = slice(h * HALF // 16, (h + 1) * HALF // 16)
+            for t in range(PACK + 1):
+                if t < PACK:
+                    nc.vector.tensor_tensor(prod[:, t, cols], bwin[t][:].indirect(n5_t[:, lcols]), th[:, t, cols], ALU.mult)
+                if t > 0:
+                    nc.vector.tensor_tensor(res[:, t - 1, cols], ga[:, t - 1, cols], prod[:, t - 1, cols], ALU.subtract)
+            nc.sync.dma_start(out_rows[:, :, cols], res[:, :, cols])
+            icols = slice(PACK * h * HALF, PACK * (h + 1) * HALF)
+            interleave(oi[:, icols], res[:, :, cols], nc.scalar.copy if h == 0 else nc.vector.tensor_copy)
+            nc.vector.quantize_mx(out=oq[:, cols].bitcast(FP8X4), scales=osc[:, cols], in_=oi[:, icols])
+            nc.sync.dma_start(out_words[:, cols], oq[:, cols].bitcast(I32))
+        for q in range(4):
+            nc.scalar.dma_start(out_2[0, 4 * q : 4 * q + 4, :].bitcast(I32), osc[32 * q : 32 * q + 4, :].bitcast(I32))

@@ -18,6 +18,8 @@ PACK = 4
 T = 2048
 S = 512
 HALF = S // 2
+VSQ = 2
+PRE = 2
 FLOPS = 3 * 2 * 512 * 512 * 512
 
 
@@ -69,91 +71,86 @@ def tile_picked_forksoftbbigshare_none_po_kernel(
             )
 
         xs = sb.tile([P, T], U8, name="xs", tag="xs", align_bytes=64)
-        w1s = sb.tile([P, S], U8, name="w1s", align_bytes=64)
+        w1s = sb.tile([P, S], U8, name="w1s", tag="w1s", align_bytes=64)
+        nc.vector.memset(w1s[:].bitcast(I32), 0)
         nc.vector.memset(xs[:].bitcast(I32), 0)
-        nc.gpsimd.memset(w1s[:].bitcast(I32), 0)
-
-        offs_t = load_list(offs, "offs_t")
-        n1_t = load_list(n1, "n1_t")
-        n2_t = load_list(n2, "n2_t")
-        n3_t = load_list(n3, "n3_t")
-        n4_t = load_list(n4, "n4_t")
-        n5_t = load_list(n5, "n5_t")
-        w1w = load_words(w1_words, "w1w", S, nc.sync, "w1w")
-        xw = load_words(x_words, "xw", T, nc.sync, "xw")
-        load_scales(xs, x_scales, 0, [nc.sync] * 4)
-        load_scales(w1s, w1_scales, 0, [nc.gpsimd, nc.sync, nc.sync, nc.sync])
-        gn_t = sb.tile([P, PACK], F32, name="gn_t")
-        nc.gpsimd.dma_start(gn_t[:], gn.rearrange("(p t) o -> p (t o)", t=PACK))
-        gm_t = sb.tile([P, PACK], F32, name="gm_t")
-        nc.gpsimd.dma_start(gm_t[:], gm.rearrange("(p t) o -> p (t o)", t=PACK))
-
-        ident = sb.tile([P, P], F32, name="ident")
-        make_identity(nc, ident[:])
-
         ywin = [sb.tile([P, 2 * S], F32, name=f"ywin{t}") for t in range(PACK)]
         for t in range(PACK):
             nc.vector.memset(ywin[t][:, S:], 0.0)
 
-        w1d = deal(w1w, "w1d", U32, I32)
+        offs_t = load_list(offs, "offs_t")
+        load_scales(w1s, w1_scales, 0, [nc.sync, nc.sync, nc.gpsimd, nc.gpsimd])
+        load_scales(xs, x_scales, 0, [nc.sync] * 4)
+        xw = load_words(x_words, "xw", T, nc.sync, "xw")
+        w1w = load_words(w1_words, "w1w", S, nc.sync, "w1w")
+        n2_t = load_list(n2, "n2_t")
+        n1_t = load_list(n1, "n1_t")
+        n3_t = load_list(n3, "n3_t")
+        gn_t = sb.tile([P, PACK], F32, name="gn_t")
+        nc.sync.dma_start(gn_t[:], gn.rearrange("(p t) o -> p (t o)", t=PACK))
+        gm_t = sb.tile([P, PACK], F32, name="gm_t")
+        nc.sync.dma_start(gm_t[:], gm.rearrange("(p t) o -> p (t o)", t=PACK))
+
+        ident = sb.tile([P, P], F32, name="ident")
+        make_identity(nc, ident[:])
+
         xgs = sb.tile([P, S], U8, name="xgs", align_bytes=64)
         nc.vector.tensor_copy(xgs[:], xs[:].indirect(offs_t[:]))
         w1sd = deal(w1s, "w1sd", U8, U8)
         xg = sb.tile([P, S], U32, name="xg", align_bytes=64)
         nc.vector.tensor_copy(xg[:], xw[:].indirect(offs_t[:]))
+        w1d = deal(w1w, "w1d", U32, I32)
 
-        w2w = load_words(w2_words, "w2w", S, nc.sync, "xw")
-        w3w = load_words(w3_words, "w3w", S, nc.sync, "w1w")
-        w23s = sb.tile([P, S], U8, name="w23s", tag="xs", align_bytes=64)
+        w2w = load_words(w2_words, "w2w", S, nc.sync, "w2w")
+        w3w = load_words(w3_words, "w3w", S, nc.sync, "w3w")
+        w23s = sb.tile([P, S], U8, name="w23s", align_bytes=64)
         nc.gpsimd.memset(w23s[:].bitcast(I32), 0)
         load_scales(w23s, w2_scales, 0, [nc.sync] * 4)
         load_scales(w23s, w3_scales, 4, [nc.sync] * 4)
+        n4_t = load_list(n4, "n4_t")
+        n5_t = load_list(n5, "n5_t")
 
         ybank = [ps.tile([P, S], F32, name=f"ybank{t}", tag=f"A{t}") for t in range(PACK)]
         for t in range(PACK):
             product(ybank[t], w1d, w1sd, 0, t, xg, xgs)
-        for t in range(PACK):
-            nc.scalar.copy(ywin[t][:, :S], ybank[t][:])
 
         ex = sb.tile([P, PACK, S], F32, name="ex")
         e2 = sb.tile([P, PACK, S], F32, name="e2")
         e3 = sb.tile([P, PACK, S], F32, name="e3")
         dbank = [ps.tile([P, PACK, P], F32, name=f"dbank{t}", tag=f"B{t}") for t in range(PACK)]
+        awin = [sb.tile([P, 2 * S], F32, name=f"awin{t}") for t in range(PACK)]
+        big = sb.tile([P, PACK, S], F32, name="big")
+        zb = sb.tile([P, PACK, S], BF16, name="zb")
+        nc.scalar.copy(ywin[0][:, :S], ybank[0][:])
         for t in range(PACK):
-            nc.scalar.activation(ex[:, t, :], ywin[t][:, :S], ACT.Exp, scale=0.5)
+            if t + 1 < PACK:
+                nc.vector.tensor_copy(ywin[t + 1][:, :S], ybank[t + 1][:])
+            nc.vector.tensor_copy(awin[t][:, S:], ywin[t][:].indirect(n1_t[:]))
+            if t > 0:
+                nc.vector.tensor_tensor(big[:, t - 1, :], awin[t - 1][:, S:], ybank[t - 1][:], ALU.max)
             nc.scalar.activation(e2[:, t, :], ywin[t][:].indirect(n2_t[:]), ACT.Exp, scale=0.5)
+            nc.scalar.activation(ex[:, t, :], ywin[t][:, :S], ACT.Exp, scale=0.5)
             nc.scalar.activation(e3[:, t, :], ywin[t][:].indirect(n3_t[:]), ACT.Exp, scale=0.5)
             for j in range(PACK):
-                for i, term in enumerate((ex, e2, e3)):
+                for i, term in enumerate((e2, ex, e3)):
                     nc.tensor.matmul(
                         dbank[t][:, j, :], lhsT=term[:, t, j * P : (j + 1) * P], rhs=ident[:],
                         is_transpose=True, start=(i == 0), stop=(i == 2),
                     )
-
-        awin = [sb.tile([P, 2 * S], F32, name=f"awin{t}") for t in range(PACK)]
-        big = sb.tile([P, PACK, S], F32, name="big")
-        zb = sb.tile([P, PACK, S], BF16, name="zb")
-        for t in range(PACK + 1):
-            if t < PACK:
-                nc.vector.tensor_copy(awin[t][:, S:], ywin[t][:].indirect(n1_t[:]))
-            if t > 0:
-                nc.vector.tensor_tensor(big[:, t - 1, :], awin[t - 1][:, S:], ybank[t - 1][:], ALU.max)
-        for t in range(PACK):
-            nc.vector.tensor_scalar(zb[:, t, :], big[:, t, :], gn_t[:, t : t + 1], None, ALU.mult)
+        nc.vector.tensor_scalar(zb[:, 0, :], big[:, 0, :], gn_t[:, 0:1], None, ALU.mult)
+        nc.vector.tensor_tensor(big[:, PACK - 1, :], awin[PACK - 1][:, S:], ybank[PACK - 1][:], ALU.max)
         w2d = deal(w2w, "w2d", U32, I32)
+        for t in range(1, PACK):
+            nc.vector.tensor_scalar(zb[:, t, :], big[:, t, :], gn_t[:, t : t + 1], None, ALU.mult)
+        w23sd = deal(w23s, "w23sd", U8, U8)
         zi = sb.tile([P, PACK * S], BF16, name="zi", align_bytes=64)
         interleave(zi[:], zb[:])
-        w23sd = deal(w23s, "w23sd", U8, U8)
+        w3d = deal(w3w, "w3d", U32, I32)
         zq = sb.tile([P, S], U32, name="zq", align_bytes=64)
         zs = sb.tile([P, S], U8, name="zs", align_bytes=64)
         nc.vector.quantize_mx(out=zq[:].bitcast(FP8X4), scales=zs[:], in_=zi[:])
-        w3d = deal(w3w, "w3d", U32, I32)
         gm2 = sb.tile([P, PACK], F32, name="gm2")
         nc.vector.tensor_scalar(gm2[:], gm_t[:], 2.0, None, ALU.mult)
-
-        abank = [ps.tile([P, S], F32, name=f"abank{t}", tag=f"A{t}") for t in range(PACK)]
-        for t in range(PACK):
-            product(abank[t], w2d, w23sd, 0, t, zq, zs)
 
         root = sb.tile([P, PACK, S], F32, name="root")
         inv = sb.tile([P, PACK, S], F32, name="inv")
@@ -161,16 +158,24 @@ def tile_picked_forksoftbbigshare_none_po_kernel(
         rbank = []
         for t in range(PACK):
             nc.scalar.activation(root[:, t, :], dbank[t][:].rearrange("p j m -> p (j m)"), ACT.Abs_reciprocal_sqrt)
-            nc.scalar.activation(inv[:, t, :], root[:, t, :], ACT.Square)
+            src = root
+            if t >= VSQ:
+                nc.scalar.activation(inv[:, t, :], root[:, t, :], ACT.Square)
+                src = inv
             bank = ps.tile([P, PACK, P], F32, name=f"rbank{t}", tag=f"B{t}")
             for j in range(PACK):
-                nc.tensor.transpose(bank[:, j, :], inv[:, t, j * P : (j + 1) * P], ident[:])
-            rbank.append(bank)
+                nc.tensor.transpose(bank[:, j, :], src[:, t, j * P : (j + 1) * P], ident[:])
+            rbank.append(bank[:].rearrange("p j m -> p (j m)"))
+        abank = [ps.tile([P, S], F32, name=f"abank{t}", tag=f"A{t}") for t in range(PACK)]
         for t in range(PACK):
-            nc.vector.scalar_tensor_tensor(
-                z2b[:, t, :], ex[:, t, :], gm2[:, t : t + 1], rbank[t][:].rearrange("p j m -> p (j m)"), ALU.mult, ALU.mult
-            )
-        z2i = sb.tile([P, PACK * S], BF16, name="z2i", align_bytes=64)
+            product(abank[t], w2d, w23sd, 0, t, zq, zs)
+        for t in range(VSQ):
+            nc.vector.scalar_tensor_tensor(inv[:, t, :], ex[:, t, :], gm2[:, t : t + 1], rbank[t], ALU.mult, ALU.mult)
+        for t in range(VSQ):
+            nc.vector.tensor_tensor(z2b[:, t, :], inv[:, t, :], rbank[t], ALU.mult)
+        for t in range(VSQ, PACK):
+            nc.vector.scalar_tensor_tensor(z2b[:, t, :], ex[:, t, :], gm2[:, t : t + 1], rbank[t], ALU.mult, ALU.mult)
+        z2i = sb.tile([P, PACK * S], BF16, name="z2i", tag="z2i", align_bytes=64)
         interleave(z2i[:], z2b[:])
         z2q = sb.tile([P, S], U32, name="z2q", align_bytes=64)
         z2s = sb.tile([P, S], U8, name="z2s", align_bytes=64)
@@ -179,18 +184,16 @@ def tile_picked_forksoftbbigshare_none_po_kernel(
         for t in range(PACK):
             product(bbank[t], w3d, w23sd, 4, t, z2q, z2s)
 
-        ga = sb.tile([P, PACK, S], F32, name="ga")
-        for t in range(PACK + 1):
-            if t < PACK:
-                nc.vector.tensor_copy(awin[t][:, :S], abank[t][:])
-            if t > 0:
-                nc.vector.tensor_copy(ga[:, t - 1, :], awin[t - 1][:].indirect(n4_t[:]))
+        for t in range(PACK):
+            nc.scalar.copy(awin[t][:, :S], abank[t][:])
+        ga = sb.tile([P, PRE, S], F32, name="ga", tag="z2i", align_bytes=64)
+        for t in range(PRE):
+            nc.vector.tensor_copy(ga[:, t, :], awin[t][:].indirect(n4_t[:]))
 
-        bwin = [sb.tile([P, S], F32, name=f"bwin{t}") for t in range(PACK)]
         th = sb.tile([P, PACK, S], F32, name="th")
         for t in range(PACK):
-            nc.scalar.copy(bwin[t][:], bbank[t][:])
             nc.scalar.activation(th[:, t, :], bbank[t][:], ACT.Tanh)
+            nc.scalar.copy(ywin[t][:, :S], bbank[t][:])
 
         prod = sb.tile([P, PACK, S], F32, name="prod")
         res = sb.tile([P, PACK, S], F32, name="res")
@@ -199,18 +202,26 @@ def tile_picked_forksoftbbigshare_none_po_kernel(
         osc = sb.tile([P, S], U8, name="osc", align_bytes=64)
         out_rows = out_0.rearrange("(p t) c -> p t c", t=PACK)
         out_words = out_1[0].rearrange("p c r -> p (c r)").bitcast(I32)
+        pieces = [(t, 0, S) for t in range(PACK - 1)] + [(PACK - 1, 0, HALF), (PACK - 1, HALF, S)]
+
+        def times_tanh(t, lo, hi):
+            nc.vector.tensor_tensor(prod[:, t, lo:hi], ywin[t][:].indirect(n5_t[:, lo // 16 : hi // 16]), th[:, t, lo:hi], ALU.mult)
+
+        def take_from_a(t, lo, hi):
+            picked = ga[:, t, lo:hi] if t < PRE else awin[t][:].indirect(n4_t[:, lo // 16 : hi // 16])
+            nc.vector.tensor_tensor(res[:, t, lo:hi], picked, prod[:, t, lo:hi], ALU.subtract)
+            nc.sync.dma_start(out_rows[:, t, lo:hi], res[:, t, lo:hi])
+
+        times_tanh(*pieces[0])
+        for k in range(1, len(pieces)):
+            times_tanh(*pieces[k])
+            take_from_a(*pieces[k - 1])
+        take_from_a(*pieces[-1])
+        interleave(oi[:, : PACK * HALF], res[:, :, :HALF], nc.scalar.copy)
+        interleave(oi[:, PACK * HALF :], res[:, :, HALF:])
         for h in range(2):
             cols = slice(h * HALF, (h + 1) * HALF)
-            lcols = slice(h * HALF // 16, (h + 1) * HALF // 16)
-            for t in range(PACK + 1):
-                if t < PACK:
-                    nc.vector.tensor_tensor(prod[:, t, cols], bwin[t][:].indirect(n5_t[:, lcols]), th[:, t, cols], ALU.mult)
-                if t > 0:
-                    nc.vector.tensor_tensor(res[:, t - 1, cols], ga[:, t - 1, cols], prod[:, t - 1, cols], ALU.subtract)
-            nc.sync.dma_start(out_rows[:, :, cols], res[:, :, cols])
-            icols = slice(PACK * h * HALF, PACK * (h + 1) * HALF)
-            interleave(oi[:, icols], res[:, :, cols], nc.scalar.copy if h == 0 else nc.vector.tensor_copy)
-            nc.vector.quantize_mx(out=oq[:, cols].bitcast(FP8X4), scales=osc[:, cols], in_=oi[:, icols])
+            nc.vector.quantize_mx(out=oq[:, cols].bitcast(FP8X4), scales=osc[:, cols], in_=oi[:, PACK * h * HALF : PACK * (h + 1) * HALF])
             nc.sync.dma_start(out_words[:, cols], oq[:, cols].bitcast(I32))
         for q in range(4):
             nc.scalar.dma_start(out_2[0, 4 * q : 4 * q + 4, :].bitcast(I32), osc[32 * q : 32 * q + 4, :].bitcast(I32))

@@ -18,8 +18,8 @@ PACK = 4
 T = 2048
 S = 512
 HALF = S // 2
-VSQ = 2
-PRE = 2
+VSQ = 1
+VGATHER = 1
 FLOPS = 3 * 2 * 512 * 512 * 512
 
 
@@ -42,9 +42,9 @@ def tile_picked_forksoftbbigshare_none_po_kernel(
             queue.dma_start(tile[:].bitcast(I32), src[0].rearrange("p c r -> p (c r)").bitcast(I32))
             return tile
 
-        def load_scales(tile, src, row, queues):
-            for q, queue in enumerate(queues):
-                queue.dma_start(
+        def load_scales(tile, src, row, quadrants=range(4)):
+            for q in quadrants:
+                nc.sync.dma_start(
                     tile[32 * q + row : 32 * q + row + 4, :].bitcast(I32),
                     src[0, 4 * q : 4 * q + 4, :].bitcast(I32),
                 )
@@ -63,29 +63,32 @@ def tile_picked_forksoftbbigshare_none_po_kernel(
                 src.rearrange("p t (c i) -> p c t i", i=4),
             )
 
-        def product(bank, words, scales, row, t, codes, code_scales):
+        def product(bank, words, scales, row, t, codes, code_scales, lo=0, hi=S):
             cols = slice(t * P, (t + 1) * P)
             nc.tensor.matmul_mx(
-                out=bank[:], lhsT=words[:, cols].bitcast(FP8X4), lhsT_scale=scales[row:P, cols],
-                rhs=codes[:].bitcast(FP8X4), rhs_scale=code_scales[:], start=True, stop=True,
+                out=bank[:, lo:hi], lhsT=words[:, cols].bitcast(FP8X4), lhsT_scale=scales[row:P, cols],
+                rhs=codes[:, lo:hi].bitcast(FP8X4), rhs_scale=code_scales[:, lo:hi], start=True, stop=True,
             )
 
         xs = sb.tile([P, T], U8, name="xs", tag="xs", align_bytes=64)
         w1s = sb.tile([P, S], U8, name="w1s", tag="w1s", align_bytes=64)
-        nc.vector.memset(w1s[:].bitcast(I32), 0)
         nc.vector.memset(xs[:].bitcast(I32), 0)
+        nc.vector.memset(w1s[:].bitcast(I32), 0)
         ywin = [sb.tile([P, 2 * S], F32, name=f"ywin{t}") for t in range(PACK)]
         for t in range(PACK):
             nc.vector.memset(ywin[t][:, S:], 0.0)
 
         offs_t = load_list(offs, "offs_t")
-        load_scales(w1s, w1_scales, 0, [nc.sync, nc.sync, nc.gpsimd, nc.gpsimd])
-        load_scales(xs, x_scales, 0, [nc.sync] * 4)
-        xw = load_words(x_words, "xw", T, nc.sync, "xw")
         w1w = load_words(w1_words, "w1w", S, nc.sync, "w1w")
+        load_scales(xs, x_scales, 0)
+        load_scales(w1s, w1_scales, 0, range(1))
+        xw = load_words(x_words, "xw", T, nc.sync, "xw")
+        load_scales(w1s, w1_scales, 0, range(1, 4))
         n2_t = load_list(n2, "n2_t")
         n1_t = load_list(n1, "n1_t")
         n3_t = load_list(n3, "n3_t")
+        w3w = load_words(w3_words, "w3w", S, nc.sync, "w3w")
+        w2w = load_words(w2_words, "w2w", S, nc.sync, "w2w")
         gn_t = sb.tile([P, PACK], F32, name="gn_t")
         nc.sync.dma_start(gn_t[:], gn.rearrange("(p t) o -> p (t o)", t=PACK))
         gm_t = sb.tile([P, PACK], F32, name="gm_t")
@@ -94,33 +97,39 @@ def tile_picked_forksoftbbigshare_none_po_kernel(
         ident = sb.tile([P, P], F32, name="ident")
         make_identity(nc, ident[:])
 
+        w1d = deal(w1w, "w1d", U32, I32)
         xgs = sb.tile([P, S], U8, name="xgs", align_bytes=64)
         nc.vector.tensor_copy(xgs[:], xs[:].indirect(offs_t[:]))
-        w1sd = deal(w1s, "w1sd", U8, U8)
         xg = sb.tile([P, S], U32, name="xg", align_bytes=64)
-        nc.vector.tensor_copy(xg[:], xw[:].indirect(offs_t[:]))
-        w1d = deal(w1w, "w1d", U32, I32)
+        w1sd = sb.tile([P, S], U8, name="w1sd", align_bytes=64)
+        w1s_from = w1s[:].rearrange("p (m t) -> p t m", t=PACK)
+        w1s_to = w1sd[:].rearrange("p (t m) -> p t m", t=PACK)
+        nc.vector.tensor_copy(xg[:, :HALF], xw[:].indirect(offs_t[:, : HALF // 16]))
+        nc.vector.tensor_copy(w1s_to[:, 0, :], w1s_from[:, 0, :])
+        nc.vector.tensor_copy(xg[:, HALF:], xw[:].indirect(offs_t[:, HALF // 16 :]))
+        nc.vector.tensor_copy(w1s_to[:, 1:, :], w1s_from[:, 1:, :])
+        w3d = deal(w3w, "w3d", U32, I32)
 
-        w2w = load_words(w2_words, "w2w", S, nc.sync, "w2w")
-        w3w = load_words(w3_words, "w3w", S, nc.sync, "w3w")
         w23s = sb.tile([P, S], U8, name="w23s", align_bytes=64)
         nc.gpsimd.memset(w23s[:].bitcast(I32), 0)
-        load_scales(w23s, w2_scales, 0, [nc.sync] * 4)
-        load_scales(w23s, w3_scales, 4, [nc.sync] * 4)
+        load_scales(w23s, w2_scales, 0)
+        load_scales(w23s, w3_scales, 4)
         n4_t = load_list(n4, "n4_t")
         n5_t = load_list(n5, "n5_t")
 
         ybank = [ps.tile([P, S], F32, name=f"ybank{t}", tag=f"A{t}") for t in range(PACK)]
-        for t in range(PACK):
+        product(ybank[0], w1d, w1sd, 0, 0, xg, xgs, 0, HALF)
+        product(ybank[0], w1d, w1sd, 0, 0, xg, xgs, HALF, S)
+        for t in range(1, PACK):
             product(ybank[t], w1d, w1sd, 0, t, xg, xgs)
 
-        ex = sb.tile([P, PACK, S], F32, name="ex")
-        e2 = sb.tile([P, PACK, S], F32, name="e2")
+        exwin = [sb.tile([P, 2 * S], F32, name=f"exwin{t}") for t in range(PACK)]
+        ex = [exwin[t][:, :S] for t in range(PACK)]
+        e2 = [exwin[t][:, S:] for t in range(PACK)]
         e3 = sb.tile([P, PACK, S], F32, name="e3")
         dbank = [ps.tile([P, PACK, P], F32, name=f"dbank{t}", tag=f"B{t}") for t in range(PACK)]
         awin = [sb.tile([P, 2 * S], F32, name=f"awin{t}") for t in range(PACK)]
         big = sb.tile([P, PACK, S], F32, name="big")
-        zb = sb.tile([P, PACK, S], BF16, name="zb")
         nc.scalar.copy(ywin[0][:, :S], ybank[0][:])
         for t in range(PACK):
             if t + 1 < PACK:
@@ -128,31 +137,25 @@ def tile_picked_forksoftbbigshare_none_po_kernel(
             nc.vector.tensor_copy(awin[t][:, S:], ywin[t][:].indirect(n1_t[:]))
             if t > 0:
                 nc.vector.tensor_tensor(big[:, t - 1, :], awin[t - 1][:, S:], ybank[t - 1][:], ALU.max)
-            nc.scalar.activation(e2[:, t, :], ywin[t][:].indirect(n2_t[:]), ACT.Exp, scale=0.5)
-            nc.scalar.activation(ex[:, t, :], ywin[t][:, :S], ACT.Exp, scale=0.5)
-            nc.scalar.activation(e3[:, t, :], ywin[t][:].indirect(n3_t[:]), ACT.Exp, scale=0.5)
+            nc.scalar.activation(e2[t], ywin[t][:].indirect(n2_t[:]), ACT.Exp, scale=0.5)
+            nc.scalar.activation(ex[t], ywin[t][:, :S], ACT.Exp, scale=0.5)
+            if t < PACK - VGATHER:
+                nc.scalar.activation(e3[:, t, :], ywin[t][:].indirect(n3_t[:]), ACT.Exp, scale=0.5)
+            else:
+                nc.vector.tensor_copy(e3[:, t, :], exwin[t][:].indirect(n3_t[:]))
             for j in range(PACK):
-                for i, term in enumerate((e2, ex, e3)):
+                for i, term in enumerate((e2[t], ex[t], e3[:, t, :])):
                     nc.tensor.matmul(
-                        dbank[t][:, j, :], lhsT=term[:, t, j * P : (j + 1) * P], rhs=ident[:],
+                        dbank[t][:, j, :], lhsT=term[:, j * P : (j + 1) * P], rhs=ident[:],
                         is_transpose=True, start=(i == 0), stop=(i == 2),
                     )
-        nc.vector.tensor_scalar(zb[:, 0, :], big[:, 0, :], gn_t[:, 0:1], None, ALU.mult)
         nc.vector.tensor_tensor(big[:, PACK - 1, :], awin[PACK - 1][:, S:], ybank[PACK - 1][:], ALU.max)
         w2d = deal(w2w, "w2d", U32, I32)
-        for t in range(1, PACK):
-            nc.vector.tensor_scalar(zb[:, t, :], big[:, t, :], gn_t[:, t : t + 1], None, ALU.mult)
         w23sd = deal(w23s, "w23sd", U8, U8)
-        zi = sb.tile([P, PACK * S], BF16, name="zi", align_bytes=64)
-        interleave(zi[:], zb[:])
-        w3d = deal(w3w, "w3d", U32, I32)
-        zq = sb.tile([P, S], U32, name="zq", align_bytes=64)
-        zs = sb.tile([P, S], U8, name="zs", align_bytes=64)
-        nc.vector.quantize_mx(out=zq[:].bitcast(FP8X4), scales=zs[:], in_=zi[:])
         gm2 = sb.tile([P, PACK], F32, name="gm2")
         nc.vector.tensor_scalar(gm2[:], gm_t[:], 2.0, None, ALU.mult)
 
-        root = sb.tile([P, PACK, S], F32, name="root")
+        root = sb.tile([P, PACK, S], F32, name="root", tag="root")
         inv = sb.tile([P, PACK, S], F32, name="inv")
         z2b = sb.tile([P, PACK, S], BF16, name="z2b")
         rbank = []
@@ -162,38 +165,43 @@ def tile_picked_forksoftbbigshare_none_po_kernel(
             if t >= VSQ:
                 nc.scalar.activation(inv[:, t, :], root[:, t, :], ACT.Square)
                 src = inv
-            bank = ps.tile([P, PACK, P], F32, name=f"rbank{t}", tag=f"B{t}")
+            bank = ps.tile([P, PACK, P], F32, name=f"rbank{t}", tag=f"A{t}")
             for j in range(PACK):
                 nc.tensor.transpose(bank[:, j, :], src[:, t, j * P : (j + 1) * P], ident[:])
             rbank.append(bank[:].rearrange("p j m -> p (j m)"))
-        abank = [ps.tile([P, S], F32, name=f"abank{t}", tag=f"A{t}") for t in range(PACK)]
+        zb = sb.tile([P, PACK, S], BF16, name="zb", tag="root")
         for t in range(PACK):
-            product(abank[t], w2d, w23sd, 0, t, zq, zs)
+            nc.scalar.activation(zb[:, t, :], big[:, t, :], ACT.Copy, scale=gn_t[:, t : t + 1])
         for t in range(VSQ):
-            nc.vector.scalar_tensor_tensor(inv[:, t, :], ex[:, t, :], gm2[:, t : t + 1], rbank[t], ALU.mult, ALU.mult)
+            nc.vector.scalar_tensor_tensor(inv[:, t, :], ex[t], gm2[:, t : t + 1], rbank[t], ALU.mult, ALU.mult)
         for t in range(VSQ):
             nc.vector.tensor_tensor(z2b[:, t, :], inv[:, t, :], rbank[t], ALU.mult)
         for t in range(VSQ, PACK):
-            nc.vector.scalar_tensor_tensor(z2b[:, t, :], ex[:, t, :], gm2[:, t : t + 1], rbank[t], ALU.mult, ALU.mult)
-        z2i = sb.tile([P, PACK * S], BF16, name="z2i", tag="z2i", align_bytes=64)
-        interleave(z2i[:], z2b[:])
-        z2q = sb.tile([P, S], U32, name="z2q", align_bytes=64)
-        z2s = sb.tile([P, S], U8, name="z2s", align_bytes=64)
-        nc.vector.quantize_mx(out=z2q[:].bitcast(FP8X4), scales=z2s[:], in_=z2i[:])
+            nc.vector.scalar_tensor_tensor(z2b[:, t, :], ex[t], gm2[:, t : t + 1], rbank[t], ALU.mult, ALU.mult)
+
+        def quantise(planes, name):
+            woven = sb.tile([P, PACK * S], BF16, name=f"{name}_woven", tag="woven", align_bytes=64)
+            interleave(woven[:], planes[:])
+            codes = sb.tile([P, S], U32, name=f"{name}_codes", align_bytes=64)
+            scales = sb.tile([P, S], U8, name=f"{name}_scales", align_bytes=64)
+            nc.vector.quantize_mx(out=codes[:].bitcast(FP8X4), scales=scales[:], in_=woven[:])
+            return codes, scales
+
+        z2q, z2s = quantise(z2b, "z2")
         bbank = [ps.tile([P, S], F32, name=f"bbank{t}", tag=f"B{t}") for t in range(PACK)]
         for t in range(PACK):
             product(bbank[t], w3d, w23sd, 4, t, z2q, z2s)
-
+        zq, zs = quantise(zb, "z")
+        abank = [ps.tile([P, S], F32, name=f"abank{t}", tag=f"A{t}") for t in range(PACK)]
         for t in range(PACK):
-            nc.scalar.copy(awin[t][:, :S], abank[t][:])
-        ga = sb.tile([P, PRE, S], F32, name="ga", tag="z2i", align_bytes=64)
-        for t in range(PRE):
-            nc.vector.tensor_copy(ga[:, t, :], awin[t][:].indirect(n4_t[:]))
+            product(abank[t], w2d, w23sd, 0, t, zq, zs)
 
         th = sb.tile([P, PACK, S], F32, name="th")
         for t in range(PACK):
             nc.scalar.activation(th[:, t, :], bbank[t][:], ACT.Tanh)
             nc.scalar.copy(ywin[t][:, :S], bbank[t][:])
+        for t in range(PACK):
+            nc.scalar.copy(awin[t][:, :S], abank[t][:])
 
         prod = sb.tile([P, PACK, S], F32, name="prod")
         res = sb.tile([P, PACK, S], F32, name="res")
@@ -202,21 +210,13 @@ def tile_picked_forksoftbbigshare_none_po_kernel(
         osc = sb.tile([P, S], U8, name="osc", align_bytes=64)
         out_rows = out_0.rearrange("(p t) c -> p t c", t=PACK)
         out_words = out_1[0].rearrange("p c r -> p (c r)").bitcast(I32)
+        for t in range(PACK):
+            nc.vector.tensor_tensor(prod[:, t, :], ywin[t][:].indirect(n5_t[:]), th[:, t, :], ALU.mult)
         pieces = [(t, 0, S) for t in range(PACK - 1)] + [(PACK - 1, 0, HALF), (PACK - 1, HALF, S)]
-
-        def times_tanh(t, lo, hi):
-            nc.vector.tensor_tensor(prod[:, t, lo:hi], ywin[t][:].indirect(n5_t[:, lo // 16 : hi // 16]), th[:, t, lo:hi], ALU.mult)
-
-        def take_from_a(t, lo, hi):
-            picked = ga[:, t, lo:hi] if t < PRE else awin[t][:].indirect(n4_t[:, lo // 16 : hi // 16])
+        for t, lo, hi in pieces:
+            picked = awin[t][:].indirect(n4_t[:, lo // 16 : hi // 16])
             nc.vector.tensor_tensor(res[:, t, lo:hi], picked, prod[:, t, lo:hi], ALU.subtract)
             nc.sync.dma_start(out_rows[:, t, lo:hi], res[:, t, lo:hi])
-
-        times_tanh(*pieces[0])
-        for k in range(1, len(pieces)):
-            times_tanh(*pieces[k])
-            take_from_a(*pieces[k - 1])
-        take_from_a(*pieces[-1])
         interleave(oi[:, : PACK * HALF], res[:, :, :HALF], nc.scalar.copy)
         interleave(oi[:, PACK * HALF :], res[:, :, HALF:])
         for h in range(2):

@@ -15,12 +15,16 @@ ACT = mybir.ActivationFunctionType
 
 P = 128
 PACK = 4
+QUADRANTS = 4
 T = 2048
 S = 512
 HALF = S // 2
-VSQ = 1
-VGATHER = 1
-FLOPS = 3 * 2 * 512 * 512 * 512
+PER_COLUMN = 16
+W3_ROW = 4
+LINE = 4
+SQUARED_ON_VECTOR = 2
+N3_ON_VECTOR = 2
+FLOPS = 3 * 2 * S * S * S
 
 
 def tile_picked_forksoftbbigshare_none_po_kernel(
@@ -33,21 +37,26 @@ def tile_picked_forksoftbbigshare_none_po_kernel(
         ps = ctx.enter_context(tc.psum_pool(name="ps", bufs=1))
 
         def load_list(src, name):
-            tile = sb.tile([P, S // 16], U16, name=name)
+            tile = sb.tile([P, S // PER_COLUMN], U16, name=name)
             nc.sync.dma_start(tile[:], src)
             return tile
 
-        def load_words(src, name, cols, queue, tag):
-            tile = sb.tile([P, cols], U32, name=name, tag=tag, align_bytes=64)
-            queue.dma_start(tile[:].bitcast(I32), src[0].rearrange("p c r -> p (c r)").bitcast(I32))
+        def load_words(src, name, cols):
+            tile = sb.tile([P, cols], U32, name=name, align_bytes=64)
+            nc.sync.dma_start(tile[:].bitcast(I32), src[0].rearrange("p c r -> p (c r)").bitcast(I32))
             return tile
 
-        def load_scales(tile, src, row, quadrants=range(4)):
+        def load_scales(tile, src, row, quadrants=range(QUADRANTS)):
             for q in quadrants:
                 nc.sync.dma_start(
                     tile[32 * q + row : 32 * q + row + 4, :].bitcast(I32),
                     src[0, 4 * q : 4 * q + 4, :].bitcast(I32),
                 )
+
+        def load_gain(src, name):
+            tile = sb.tile([P, PACK], F32, name=name)
+            nc.sync.dma_start(tile[:], src.rearrange("(p t) o -> p (t o)", t=PACK))
+            return tile
 
         def deal(src, name, dtype, view):
             tile = sb.tile([P, S], dtype, name=name, align_bytes=64)
@@ -57,10 +66,10 @@ def tile_picked_forksoftbbigshare_none_po_kernel(
             )
             return tile
 
-        def interleave(dst, src, copy=nc.vector.tensor_copy):
+        def weave(dst, planes, copy=nc.vector.tensor_copy):
             copy(
-                dst.rearrange("p (c i t) -> p c t i", i=4, t=PACK),
-                src.rearrange("p t (c i) -> p c t i", i=4),
+                dst.rearrange("p (c i t) -> p c t i", i=LINE, t=PACK),
+                planes.rearrange("p t (c i) -> p c t i", i=LINE),
             )
 
         def product(bank, words, scales, row, t, codes, code_scales, lo=0, hi=S):
@@ -70,158 +79,167 @@ def tile_picked_forksoftbbigshare_none_po_kernel(
                 rhs=codes[:, lo:hi].bitcast(FP8X4), rhs_scale=code_scales[:, lo:hi], start=True, stop=True,
             )
 
-        xs = sb.tile([P, T], U8, name="xs", tag="xs", align_bytes=64)
-        w1s = sb.tile([P, S], U8, name="w1s", tag="w1s", align_bytes=64)
-        nc.vector.memset(xs[:].bitcast(I32), 0)
-        nc.vector.memset(w1s[:].bitcast(I32), 0)
-        ywin = [sb.tile([P, 2 * S], F32, name=f"ywin{t}") for t in range(PACK)]
+        x_sc = sb.tile([P, T], U8, name="x_sc", align_bytes=64)
+        w1_sc = sb.tile([P, S], U8, name="w1_sc", align_bytes=64)
+        nc.vector.memset(x_sc[:].bitcast(I32), 0)
+        nc.vector.memset(w1_sc[:].bitcast(I32), 0)
+        y_win = [sb.tile([P, 2 * S], F32, name=f"y_win{t}") for t in range(PACK)]
         for t in range(PACK):
-            nc.vector.memset(ywin[t][:, S:], 0.0)
+            nc.vector.memset(y_win[t][:, S:], 0.0)
 
         offs_t = load_list(offs, "offs_t")
-        w1w = load_words(w1_words, "w1w", S, nc.sync, "w1w")
-        load_scales(xs, x_scales, 0)
-        load_scales(w1s, w1_scales, 0, range(1))
-        xw = load_words(x_words, "xw", T, nc.sync, "xw")
-        load_scales(w1s, w1_scales, 0, range(1, 4))
+        w1_w = load_words(w1_words, "w1_w", S)
+        load_scales(x_sc, x_scales, 0)
+        load_scales(w1_sc, w1_scales, 0, range(1))
+        x_w = load_words(x_words, "x_w", T)
+        load_scales(w1_sc, w1_scales, 0, range(1, QUADRANTS))
         n2_t = load_list(n2, "n2_t")
         n1_t = load_list(n1, "n1_t")
         n3_t = load_list(n3, "n3_t")
-        w3w = load_words(w3_words, "w3w", S, nc.sync, "w3w")
-        w2w = load_words(w2_words, "w2w", S, nc.sync, "w2w")
-        gn_t = sb.tile([P, PACK], F32, name="gn_t")
-        nc.sync.dma_start(gn_t[:], gn.rearrange("(p t) o -> p (t o)", t=PACK))
-        gm_t = sb.tile([P, PACK], F32, name="gm_t")
-        nc.sync.dma_start(gm_t[:], gm.rearrange("(p t) o -> p (t o)", t=PACK))
+        w3_w = load_words(w3_words, "w3_w", S)
+        w2_w = load_words(w2_words, "w2_w", S)
+        gn_t = load_gain(gn, "gn_t")
+        gm_t = load_gain(gm, "gm_t")
 
         ident = sb.tile([P, P], F32, name="ident")
         make_identity(nc, ident[:])
 
-        w1d = deal(w1w, "w1d", U32, I32)
-        xgs = sb.tile([P, S], U8, name="xgs", align_bytes=64)
-        nc.vector.tensor_copy(xgs[:], xs[:].indirect(offs_t[:]))
-        xg = sb.tile([P, S], U32, name="xg", align_bytes=64)
-        w1sd = sb.tile([P, S], U8, name="w1sd", align_bytes=64)
-        w1s_from = w1s[:].rearrange("p (m t) -> p t m", t=PACK)
-        w1s_to = w1sd[:].rearrange("p (t m) -> p t m", t=PACK)
-        nc.vector.tensor_copy(xg[:, :HALF], xw[:].indirect(offs_t[:, : HALF // 16]))
-        nc.vector.tensor_copy(w1s_to[:, 0, :], w1s_from[:, 0, :])
-        nc.vector.tensor_copy(xg[:, HALF:], xw[:].indirect(offs_t[:, HALF // 16 :]))
-        nc.vector.tensor_copy(w1s_to[:, 1:, :], w1s_from[:, 1:, :])
-        w3d = deal(w3w, "w3d", U32, I32)
+        w1_d = deal(w1_w, "w1_d", U32, I32)
+        picked_sc = sb.tile([P, S], U8, name="picked_sc", align_bytes=64)
+        nc.vector.tensor_copy(picked_sc[:], x_sc[:].indirect(offs_t[:]))
+        picked_w = sb.tile([P, S], U32, name="picked_w", align_bytes=64)
+        w1_sd = sb.tile([P, S], U8, name="w1_sd", align_bytes=64)
+        w1_sc_from = w1_sc[:].rearrange("p (m t) -> p t m", t=PACK)
+        w1_sc_to = w1_sd[:].rearrange("p (t m) -> p t m", t=PACK)
+        nc.vector.tensor_copy(picked_w[:, :HALF], x_w[:].indirect(offs_t[:, : HALF // PER_COLUMN]))
+        nc.vector.tensor_copy(w1_sc_to[:, 0, :], w1_sc_from[:, 0, :])
+        nc.vector.tensor_copy(picked_w[:, HALF:], x_w[:].indirect(offs_t[:, HALF // PER_COLUMN :]))
+        nc.vector.tensor_copy(w1_sc_to[:, 1:, :], w1_sc_from[:, 1:, :])
+        w3_d = deal(w3_w, "w3_d", U32, I32)
 
-        w23s = sb.tile([P, S], U8, name="w23s", align_bytes=64)
-        nc.gpsimd.memset(w23s[:].bitcast(I32), 0)
-        load_scales(w23s, w2_scales, 0)
-        load_scales(w23s, w3_scales, 4)
+        w23_sc = sb.tile([P, S], U8, name="w23_sc", align_bytes=64)
+        nc.gpsimd.memset(w23_sc[:].bitcast(I32), 0)
+        load_scales(w23_sc, w2_scales, 0)
+        load_scales(w23_sc, w3_scales, W3_ROW)
         n4_t = load_list(n4, "n4_t")
         n5_t = load_list(n5, "n5_t")
 
-        ybank = [ps.tile([P, S], F32, name=f"ybank{t}", tag=f"A{t}") for t in range(PACK)]
-        product(ybank[0], w1d, w1sd, 0, 0, xg, xgs, 0, HALF)
-        product(ybank[0], w1d, w1sd, 0, 0, xg, xgs, HALF, S)
+        y_bank = [ps.tile([P, S], F32, name=f"y_bank{t}", tag=f"A{t}") for t in range(PACK)]
+        product(y_bank[0], w1_d, w1_sd, 0, 0, picked_w, picked_sc, 0, HALF)
+        product(y_bank[0], w1_d, w1_sd, 0, 0, picked_w, picked_sc, HALF, S)
         for t in range(1, PACK):
-            product(ybank[t], w1d, w1sd, 0, t, xg, xgs)
+            product(y_bank[t], w1_d, w1_sd, 0, t, picked_w, picked_sc)
 
-        exwin = [sb.tile([P, 2 * S], F32, name=f"exwin{t}") for t in range(PACK)]
-        ex = [exwin[t][:, :S] for t in range(PACK)]
-        e2 = [exwin[t][:, S:] for t in range(PACK)]
-        e3 = sb.tile([P, PACK, S], F32, name="e3")
-        dbank = [ps.tile([P, PACK, P], F32, name=f"dbank{t}", tag=f"B{t}") for t in range(PACK)]
-        awin = [sb.tile([P, 2 * S], F32, name=f"awin{t}") for t in range(PACK)]
-        big = sb.tile([P, PACK, S], F32, name="big")
-        nc.scalar.copy(ywin[0][:, :S], ybank[0][:])
-        for t in range(PACK):
-            if t + 1 < PACK:
-                nc.vector.tensor_copy(ywin[t + 1][:, :S], ybank[t + 1][:])
-            nc.vector.tensor_copy(awin[t][:, S:], ywin[t][:].indirect(n1_t[:]))
-            if t > 0:
-                nc.vector.tensor_tensor(big[:, t - 1, :], awin[t - 1][:, S:], ybank[t - 1][:], ALU.max)
-            nc.scalar.activation(e2[t], ywin[t][:].indirect(n2_t[:]), ACT.Exp, scale=0.5)
-            nc.scalar.activation(ex[t], ywin[t][:, :S], ACT.Exp, scale=0.5)
-            if t < PACK - VGATHER:
-                nc.scalar.activation(e3[:, t, :], ywin[t][:].indirect(n3_t[:]), ACT.Exp, scale=0.5)
-            else:
-                nc.vector.tensor_copy(e3[:, t, :], exwin[t][:].indirect(n3_t[:]))
-            for j in range(PACK):
-                for i, term in enumerate((e2[t], ex[t], e3[:, t, :])):
+        ex_win = [sb.tile([P, 2 * S], F32, name=f"ex_win{t}") for t in range(PACK)]
+        ex = [ex_win[t][:, :S] for t in range(PACK)]
+        ex_n2 = [ex_win[t][:, S:] for t in range(PACK)]
+        ex_n3 = sb.tile([P, PACK, S], F32, name="ex_n3")
+        d_bank = [ps.tile([P, PACK, P], F32, name=f"d_bank{t}", tag=f"B{t}") for t in range(PACK)]
+        a_win = [sb.tile([P, 2 * S], F32, name=f"a_win{t}") for t in range(PACK)]
+        y_n1 = [a_win[t][:, S:] for t in range(PACK)]
+        larger = sb.tile([P, PACK, S], F32, name="larger")
+
+        def denominator(t):
+            for j in range(S // P):
+                for i, term in enumerate((ex_n2[t], ex[t], ex_n3[:, t, :])):
                     nc.tensor.matmul(
-                        dbank[t][:, j, :], lhsT=term[:, j * P : (j + 1) * P], rhs=ident[:],
+                        d_bank[t][:, j, :], lhsT=term[:, j * P : (j + 1) * P], rhs=ident[:],
                         is_transpose=True, start=(i == 0), stop=(i == 2),
                     )
-        nc.vector.tensor_tensor(big[:, PACK - 1, :], awin[PACK - 1][:, S:], ybank[PACK - 1][:], ALU.max)
-        w2d = deal(w2w, "w2d", U32, I32)
-        w23sd = deal(w23s, "w23sd", U8, U8)
-        gm2 = sb.tile([P, PACK], F32, name="gm2")
-        nc.vector.tensor_scalar(gm2[:], gm_t[:], 2.0, None, ALU.mult)
+
+        nc.scalar.copy(y_win[0][:, :S], y_bank[0][:])
+        for t in range(PACK):
+            if t + 1 < PACK:
+                nc.vector.tensor_copy(y_win[t + 1][:, :S], y_bank[t + 1][:])
+            nc.vector.tensor_copy(y_n1[t], y_win[t][:].indirect(n1_t[:]))
+            if t > 0:
+                nc.vector.tensor_tensor(larger[:, t - 1, :], y_n1[t - 1], y_bank[t - 1][:], ALU.max)
+            nc.scalar.activation(ex_n2[t], y_win[t][:].indirect(n2_t[:]), ACT.Exp, scale=0.5)
+            nc.scalar.activation(ex[t], y_win[t][:, :S], ACT.Exp, scale=0.5)
+            if t < PACK - N3_ON_VECTOR:
+                nc.scalar.activation(ex_n3[:, t, :], y_win[t][:].indirect(n3_t[:]), ACT.Exp, scale=0.5)
+                denominator(t)
+        nc.vector.tensor_tensor(larger[:, PACK - 1, :], y_n1[PACK - 1], y_bank[PACK - 1][:], ALU.max)
+        for t in range(PACK - N3_ON_VECTOR, PACK):
+            nc.vector.tensor_copy(ex_n3[:, t, :], ex_win[t][:].indirect(n3_t[:]))
+            denominator(t)
+        w2_d = deal(w2_w, "w2_d", U32, I32)
+        w23_sd = deal(w23_sc, "w23_sd", U8, U8)
+        gm_twice = sb.tile([P, PACK], F32, name="gm_twice")
+        nc.vector.tensor_scalar(gm_twice[:], gm_t[:], 2.0, None, ALU.mult)
 
         root = sb.tile([P, PACK, S], F32, name="root", tag="root")
-        inv = sb.tile([P, PACK, S], F32, name="inv")
-        z2b = sb.tile([P, PACK, S], BF16, name="z2b")
-        rbank = []
+        step = sb.tile([P, PACK, S], F32, name="step")
+        z2_planes = sb.tile([P, PACK, S], BF16, name="z2_planes")
+        factor = []
         for t in range(PACK):
-            nc.scalar.activation(root[:, t, :], dbank[t][:].rearrange("p j m -> p (j m)"), ACT.Abs_reciprocal_sqrt)
-            src = root
-            if t >= VSQ:
-                nc.scalar.activation(inv[:, t, :], root[:, t, :], ACT.Square)
-                src = inv
-            bank = ps.tile([P, PACK, P], F32, name=f"rbank{t}", tag=f"A{t}")
-            for j in range(PACK):
-                nc.tensor.transpose(bank[:, j, :], src[:, t, j * P : (j + 1) * P], ident[:])
-            rbank.append(bank[:].rearrange("p j m -> p (j m)"))
-        zb = sb.tile([P, PACK, S], BF16, name="zb", tag="root")
+            nc.scalar.activation(root[:, t, :], d_bank[t][:].rearrange("p j m -> p (j m)"), ACT.Abs_reciprocal_sqrt)
+            turned = root
+            if t >= SQUARED_ON_VECTOR:
+                nc.scalar.activation(step[:, t, :], root[:, t, :], ACT.Square)
+                turned = step
+            bank = ps.tile([P, S // P, P], F32, name=f"factor{t}", tag=f"A{t}")
+            for j in range(S // P):
+                nc.tensor.transpose(bank[:, j, :], turned[:, t, j * P : (j + 1) * P], ident[:])
+            factor.append(bank[:].rearrange("p j m -> p (j m)"))
+
+        z_planes = sb.tile([P, PACK, S], BF16, name="z_planes", tag="root")
         for t in range(PACK):
-            nc.scalar.activation(zb[:, t, :], big[:, t, :], ACT.Copy, scale=gn_t[:, t : t + 1])
-        for t in range(VSQ):
-            nc.vector.scalar_tensor_tensor(inv[:, t, :], ex[t], gm2[:, t : t + 1], rbank[t], ALU.mult, ALU.mult)
-        for t in range(VSQ):
-            nc.vector.tensor_tensor(z2b[:, t, :], inv[:, t, :], rbank[t], ALU.mult)
-        for t in range(VSQ, PACK):
-            nc.vector.scalar_tensor_tensor(z2b[:, t, :], ex[t], gm2[:, t : t + 1], rbank[t], ALU.mult, ALU.mult)
+            nc.scalar.activation(z_planes[:, t, :], larger[:, t, :], ACT.Copy, scale=gn_t[:, t : t + 1])
+        for t in range(SQUARED_ON_VECTOR):
+            nc.vector.scalar_tensor_tensor(step[:, t, :], ex[t], gm_twice[:, t : t + 1], factor[t], ALU.mult, ALU.mult)
+        for t in range(SQUARED_ON_VECTOR):
+            nc.vector.tensor_tensor(z2_planes[:, t, :], step[:, t, :], factor[t], ALU.mult)
+        for t in range(SQUARED_ON_VECTOR, PACK):
+            nc.vector.scalar_tensor_tensor(z2_planes[:, t, :], ex[t], gm_twice[:, t : t + 1], factor[t], ALU.mult, ALU.mult)
 
         def quantise(planes, name):
             woven = sb.tile([P, PACK * S], BF16, name=f"{name}_woven", tag="woven", align_bytes=64)
-            interleave(woven[:], planes[:])
+            weave(woven[:], planes[:])
             codes = sb.tile([P, S], U32, name=f"{name}_codes", align_bytes=64)
             scales = sb.tile([P, S], U8, name=f"{name}_scales", align_bytes=64)
             nc.vector.quantize_mx(out=codes[:].bitcast(FP8X4), scales=scales[:], in_=woven[:])
             return codes, scales
 
-        z2q, z2s = quantise(z2b, "z2")
-        bbank = [ps.tile([P, S], F32, name=f"bbank{t}", tag=f"B{t}") for t in range(PACK)]
+        z2_w, z2_sc = quantise(z2_planes, "z2")
+        b_bank = [ps.tile([P, S], F32, name=f"b_bank{t}", tag=f"B{t}") for t in range(PACK)]
         for t in range(PACK):
-            product(bbank[t], w3d, w23sd, 4, t, z2q, z2s)
-        zq, zs = quantise(zb, "z")
-        abank = [ps.tile([P, S], F32, name=f"abank{t}", tag=f"A{t}") for t in range(PACK)]
+            product(b_bank[t], w3_d, w23_sd, W3_ROW, t, z2_w, z2_sc)
+        z_w, z_sc = quantise(z_planes, "z")
+        a_bank = [ps.tile([P, S], F32, name=f"a_bank{t}", tag=f"A{t}") for t in range(PACK)]
         for t in range(PACK):
-            product(abank[t], w2d, w23sd, 0, t, zq, zs)
+            product(a_bank[t], w2_d, w23_sd, 0, t, z_w, z_sc)
 
-        th = sb.tile([P, PACK, S], F32, name="th")
+        b_win = y_win
+        tanh_b = sb.tile([P, PACK, S], F32, name="tanh_b")
         for t in range(PACK):
-            nc.scalar.activation(th[:, t, :], bbank[t][:], ACT.Tanh)
-            nc.scalar.copy(ywin[t][:, :S], bbank[t][:])
+            nc.scalar.activation(tanh_b[:, t, :], b_bank[t][:], ACT.Tanh)
+            nc.scalar.copy(b_win[t][:, :S], b_bank[t][:])
         for t in range(PACK):
-            nc.scalar.copy(awin[t][:, :S], abank[t][:])
+            nc.scalar.copy(a_win[t][:, :S], a_bank[t][:])
 
-        prod = sb.tile([P, PACK, S], F32, name="prod")
-        res = sb.tile([P, PACK, S], F32, name="res")
-        oi = sb.tile([P, PACK * S], BF16, name="oi", align_bytes=64)
-        oq = sb.tile([P, S], U32, name="oq", align_bytes=64)
-        osc = sb.tile([P, S], U8, name="osc", align_bytes=64)
+        term_b = sb.tile([P, PACK, S], F32, name="term_b")
+        result = sb.tile([P, PACK, S], F32, name="result")
+        out_woven = sb.tile([P, PACK * S], BF16, name="out_woven", align_bytes=64)
+        out_w = sb.tile([P, S], U32, name="out_w", align_bytes=64)
+        out_sc = sb.tile([P, S], U8, name="out_sc", align_bytes=64)
         out_rows = out_0.rearrange("(p t) c -> p t c", t=PACK)
         out_words = out_1[0].rearrange("p c r -> p (c r)").bitcast(I32)
         for t in range(PACK):
-            nc.vector.tensor_tensor(prod[:, t, :], ywin[t][:].indirect(n5_t[:]), th[:, t, :], ALU.mult)
+            nc.vector.tensor_tensor(term_b[:, t, :], b_win[t][:].indirect(n5_t[:]), tanh_b[:, t, :], ALU.mult)
+
         pieces = [(t, 0, S) for t in range(PACK - 1)] + [(PACK - 1, 0, HALF), (PACK - 1, HALF, S)]
         for t, lo, hi in pieces:
-            picked = awin[t][:].indirect(n4_t[:, lo // 16 : hi // 16])
-            nc.vector.tensor_tensor(res[:, t, lo:hi], picked, prod[:, t, lo:hi], ALU.subtract)
-            nc.sync.dma_start(out_rows[:, t, lo:hi], res[:, t, lo:hi])
-        interleave(oi[:, : PACK * HALF], res[:, :, :HALF], nc.scalar.copy)
-        interleave(oi[:, PACK * HALF :], res[:, :, HALF:])
-        for h in range(2):
-            cols = slice(h * HALF, (h + 1) * HALF)
-            nc.vector.quantize_mx(out=oq[:, cols].bitcast(FP8X4), scales=osc[:, cols], in_=oi[:, PACK * h * HALF : PACK * (h + 1) * HALF])
-            nc.sync.dma_start(out_words[:, cols], oq[:, cols].bitcast(I32))
-        for q in range(4):
-            nc.scalar.dma_start(out_2[0, 4 * q : 4 * q + 4, :].bitcast(I32), osc[32 * q : 32 * q + 4, :].bitcast(I32))
+            a_n4 = a_win[t][:].indirect(n4_t[:, lo // PER_COLUMN : hi // PER_COLUMN])
+            nc.vector.tensor_tensor(result[:, t, lo:hi], a_n4, term_b[:, t, lo:hi], ALU.subtract)
+            nc.sync.dma_start(out_rows[:, t, lo:hi], result[:, t, lo:hi])
+        weave(out_woven[:, : PACK * HALF], result[:, :, :HALF], nc.scalar.copy)
+        weave(out_woven[:, PACK * HALF :], result[:, :, HALF:])
+        for lo in (0, HALF):
+            cols = slice(lo, lo + HALF)
+            nc.vector.quantize_mx(
+                out=out_w[:, cols].bitcast(FP8X4), scales=out_sc[:, cols], in_=out_woven[:, PACK * lo : PACK * (lo + HALF)]
+            )
+            nc.sync.dma_start(out_words[:, cols], out_w[:, cols].bitcast(I32))
+        for q in range(QUADRANTS):
+            nc.scalar.dma_start(out_2[0, 4 * q : 4 * q + 4, :].bitcast(I32), out_sc[32 * q : 32 * q + 4, :].bitcast(I32))

@@ -58,9 +58,9 @@ def tile_picked_forksoftbbigshare_none_po_kernel(
             nc.sync.dma_start(tile[:], src.rearrange("(p t) o -> p (t o)", t=PACK))
             return tile
 
-        def deal(src, name, dtype, view):
+        def deal(src, name, dtype, view, engine=nc.vector):
             tile = sb.tile([P, S], dtype, name=name, align_bytes=64)
-            nc.vector.tensor_copy(
+            engine.tensor_copy(
                 tile[:].bitcast(view).rearrange("p (t m) -> p t m", t=PACK),
                 src[:].bitcast(view).rearrange("p (m t) -> p t m", t=PACK),
             )
@@ -163,8 +163,8 @@ def tile_picked_forksoftbbigshare_none_po_kernel(
         for t in range(PACK - N3_ON_VECTOR, PACK):
             nc.vector.tensor_copy(ex_n3[:, t, :], ex_win[t][:].indirect(n3_t[:]))
             denominator(t)
-        w2_d = deal(w2_w, "w2_d", U32, I32)
-        w23_sd = deal(w23_sc, "w23_sd", U8, U8)
+        w2_d = deal(w2_w, "w2_d", U32, I32, nc.gpsimd)
+        w23_sd = deal(w23_sc, "w23_sd", U8, U8, nc.gpsimd)
         gm_twice = sb.tile([P, PACK], F32, name="gm_twice")
         nc.vector.tensor_scalar(gm_twice[:], gm_t[:], 2.0, None, ALU.mult)
 

from contextlib import ExitStack

import concourse.mybir as mybir
from concourse.masks import make_identity

F32 = mybir.dt.float32
BF16 = mybir.dt.bfloat16
I32 = mybir.dt.int32
U32 = mybir.dt.uint32
U16 = mybir.dt.uint16
U8 = mybir.dt.uint8
FP8X4 = mybir.dt.float8_e4m3fn_x4
ALU = mybir.AluOpType
ACT = mybir.ActivationFunctionType

P = 128
PACK = 4
QUADRANTS = 4
T = 2048
S = 512
HALF = S // 2
PER_COLUMN = 16
W3_ROW = 4
LINE = 4
SQUARED_ON_VECTOR = 2
N3_ON_VECTOR = 2
FLOPS = 3 * 2 * S * S * S


def tile_picked_forksoftbbigshare_none_po_kernel(
    tc, x_words, x_scales, w1_words, w1_scales, gn, w2_words, w2_scales, gm, w3_words, w3_scales,
    offs, n1, n2, n3, n4, n5, out_0, out_1, out_2,
):
    nc = tc.nc
    with ExitStack() as ctx:
        sb = ctx.enter_context(tc.tile_pool(name="sb", bufs=1))
        ps = ctx.enter_context(tc.psum_pool(name="ps", bufs=1))

        def load_list(src, name):
            tile = sb.tile([P, S // PER_COLUMN], U16, name=name)
            nc.sync.dma_start(tile[:], src)
            return tile

        def load_words(src, name, cols):
            tile = sb.tile([P, cols], U32, name=name, align_bytes=64)
            nc.sync.dma_start(tile[:].bitcast(I32), src[0].rearrange("p c r -> p (c r)").bitcast(I32))
            return tile

        def load_scales(tile, src, row, quadrants=range(QUADRANTS)):
            for q in quadrants:
                nc.sync.dma_start(
                    tile[32 * q + row : 32 * q + row + 4, :].bitcast(I32),
                    src[0, 4 * q : 4 * q + 4, :].bitcast(I32),
                )

        def load_gain(src, name):
            tile = sb.tile([P, PACK], F32, name=name)
            nc.sync.dma_start(tile[:], src.rearrange("(p t) o -> p (t o)", t=PACK))
            return tile

        def deal(src, name, dtype, view, engine=nc.vector):
            tile = sb.tile([P, S], dtype, name=name, align_bytes=64)
            engine.tensor_copy(
                tile[:].bitcast(view).rearrange("p (t m) -> p t m", t=PACK),
                src[:].bitcast(view).rearrange("p (m t) -> p t m", t=PACK),
            )
            return tile

        def weave(dst, planes, copy=nc.vector.tensor_copy):
            copy(
                dst.rearrange("p (c i t) -> p c t i", i=LINE, t=PACK),
                planes.rearrange("p t (c i) -> p c t i", i=LINE),
            )

        def product(bank, words, scales, row, t, codes, code_scales, lo=0, hi=S):
            cols = slice(t * P, (t + 1) * P)
            nc.tensor.matmul_mx(
                out=bank[:, lo:hi], lhsT=words[:, cols].bitcast(FP8X4), lhsT_scale=scales[row:P, cols],
                rhs=codes[:, lo:hi].bitcast(FP8X4), rhs_scale=code_scales[:, lo:hi], start=True, stop=True,
            )

        x_sc = sb.tile([P, T], U8, name="x_sc", align_bytes=64)
        w1_sc = sb.tile([P, S], U8, name="w1_sc", align_bytes=64)
        nc.vector.memset(x_sc[:].bitcast(I32), 0)
        nc.vector.memset(w1_sc[:].bitcast(I32), 0)
        y_win = [sb.tile([P, 2 * S], F32, name=f"y_win{t}") for t in range(PACK)]
        for t in range(PACK):
            nc.vector.memset(y_win[t][:, S:], 0.0)

        offs_t = load_list(offs, "offs_t")
        w1_w = load_words(w1_words, "w1_w", S)
        load_scales(x_sc, x_scales, 0)
        load_scales(w1_sc, w1_scales, 0, range(1))
        x_w = load_words(x_words, "x_w", T)
        load_scales(w1_sc, w1_scales, 0, range(1, QUADRANTS))
        n2_t = load_list(n2, "n2_t")
        n1_t = load_list(n1, "n1_t")
        n3_t = load_list(n3, "n3_t")
        w3_w = load_words(w3_words, "w3_w", S)
        w2_w = load_words(w2_words, "w2_w", S)
        gn_t = load_gain(gn, "gn_t")
        gm_t = load_gain(gm, "gm_t")

        ident = sb.tile([P, P], F32, name="ident")
        make_identity(nc, ident[:])

        w1_d = deal(w1_w, "w1_d", U32, I32)
        picked_sc = sb.tile([P, S], U8, name="picked_sc", align_bytes=64)
        nc.vector.tensor_copy(picked_sc[:], x_sc[:].indirect(offs_t[:]))
        picked_w = sb.tile([P, S], U32, name="picked_w", align_bytes=64)
        w1_sd = sb.tile([P, S], U8, name="w1_sd", align_bytes=64)
        w1_sc_from = w1_sc[:].rearrange("p (m t) -> p t m", t=PACK)
        w1_sc_to = w1_sd[:].rearrange("p (t m) -> p t m", t=PACK)
        nc.vector.tensor_copy(picked_w[:, :HALF], x_w[:].indirect(offs_t[:, : HALF // PER_COLUMN]))
        nc.vector.tensor_copy(w1_sc_to[:, 0, :], w1_sc_from[:, 0, :])
        nc.vector.tensor_copy(picked_w[:, HALF:], x_w[:].indirect(offs_t[:, HALF // PER_COLUMN :]))
        nc.vector.tensor_copy(w1_sc_to[:, 1:, :], w1_sc_from[:, 1:, :])
        w3_d = deal(w3_w, "w3_d", U32, I32)

        w23_sc = sb.tile([P, S], U8, name="w23_sc", align_bytes=64)
        nc.gpsimd.memset(w23_sc[:].bitcast(I32), 0)
        load_scales(w23_sc, w2_scales, 0)
        load_scales(w23_sc, w3_scales, W3_ROW)
        n4_t = load_list(n4, "n4_t")
        n5_t = load_list(n5, "n5_t")

        y_bank = [ps.tile([P, S], F32, name=f"y_bank{t}", tag=f"A{t}") for t in range(PACK)]
        product(y_bank[0], w1_d, w1_sd, 0, 0, picked_w, picked_sc, 0, HALF)
        product(y_bank[0], w1_d, w1_sd, 0, 0, picked_w, picked_sc, HALF, S)
        for t in range(1, PACK):
            product(y_bank[t], w1_d, w1_sd, 0, t, picked_w, picked_sc)

        ex_win = [sb.tile([P, 2 * S], F32, name=f"ex_win{t}") for t in range(PACK)]
        ex = [ex_win[t][:, :S] for t in range(PACK)]
        ex_n2 = [ex_win[t][:, S:] for t in range(PACK)]
        ex_n3 = sb.tile([P, PACK, S], F32, name="ex_n3")
        d_bank = [ps.tile([P, PACK, P], F32, name=f"d_bank{t}", tag=f"B{t}") for t in range(PACK)]
        a_win = [sb.tile([P, 2 * S], F32, name=f"a_win{t}") for t in range(PACK)]
        y_n1 = [a_win[t][:, S:] for t in range(PACK)]
        larger = sb.tile([P, PACK, S], F32, name="larger")

        def denominator(t):
            for j in range(S // P):
                for i, term in enumerate((ex_n2[t], ex[t], ex_n3[:, t, :])):
                    nc.tensor.matmul(
                        d_bank[t][:, j, :], lhsT=term[:, j * P : (j + 1) * P], rhs=ident[:],
                        is_transpose=True, start=(i == 0), stop=(i == 2),
                    )

        nc.scalar.copy(y_win[0][:, :S], y_bank[0][:])
        for t in range(PACK):
            if t + 1 < PACK:
                nc.vector.tensor_copy(y_win[t + 1][:, :S], y_bank[t + 1][:])
            nc.vector.tensor_copy(y_n1[t], y_win[t][:].indirect(n1_t[:]))
            if t > 0:
                nc.vector.tensor_tensor(larger[:, t - 1, :], y_n1[t - 1], y_bank[t - 1][:], ALU.max)
            nc.scalar.activation(ex_n2[t], y_win[t][:].indirect(n2_t[:]), ACT.Exp, scale=0.5)
            nc.scalar.activation(ex[t], y_win[t][:, :S], ACT.Exp, scale=0.5)
            if t < PACK - N3_ON_VECTOR:
                nc.scalar.activation(ex_n3[:, t, :], y_win[t][:].indirect(n3_t[:]), ACT.Exp, scale=0.5)
                denominator(t)
        nc.vector.tensor_tensor(larger[:, PACK - 1, :], y_n1[PACK - 1], y_bank[PACK - 1][:], ALU.max)
        for t in range(PACK - N3_ON_VECTOR, PACK):
            nc.vector.tensor_copy(ex_n3[:, t, :], ex_win[t][:].indirect(n3_t[:]))
            denominator(t)
        w2_d = deal(w2_w, "w2_d", U32, I32, nc.gpsimd)
        w23_sd = deal(w23_sc, "w23_sd", U8, U8, nc.gpsimd)
        gm_twice = sb.tile([P, PACK], F32, name="gm_twice")
        nc.vector.tensor_scalar(gm_twice[:], gm_t[:], 2.0, None, ALU.mult)

        root = sb.tile([P, PACK, S], F32, name="root", tag="root")
        step = sb.tile([P, PACK, S], F32, name="step")
        z2_planes = sb.tile([P, PACK, S], BF16, name="z2_planes")
        factor = []
        for t in range(PACK):
            nc.scalar.activation(root[:, t, :], d_bank[t][:].rearrange("p j m -> p (j m)"), ACT.Abs_reciprocal_sqrt)
            turned = root
            if t >= SQUARED_ON_VECTOR:
                nc.scalar.activation(step[:, t, :], root[:, t, :], ACT.Square)
                turned = step
            bank = ps.tile([P, S // P, P], F32, name=f"factor{t}", tag=f"A{t}")
            for j in range(S // P):
                nc.tensor.transpose(bank[:, j, :], turned[:, t, j * P : (j + 1) * P], ident[:])
            factor.append(bank[:].rearrange("p j m -> p (j m)"))

        z_planes = sb.tile([P, PACK, S], BF16, name="z_planes", tag="root")
        for t in range(PACK):
            nc.scalar.activation(z_planes[:, t, :], larger[:, t, :], ACT.Copy, scale=gn_t[:, t : t + 1])
        for t in range(SQUARED_ON_VECTOR):
            nc.vector.scalar_tensor_tensor(step[:, t, :], ex[t], gm_twice[:, t : t + 1], factor[t], ALU.mult, ALU.mult)
        for t in range(SQUARED_ON_VECTOR):
            nc.vector.tensor_tensor(z2_planes[:, t, :], step[:, t, :], factor[t], ALU.mult)
        for t in range(SQUARED_ON_VECTOR, PACK):
            nc.vector.scalar_tensor_tensor(z2_planes[:, t, :], ex[t], gm_twice[:, t : t + 1], factor[t], ALU.mult, ALU.mult)

        def quantise(planes, name):
            woven = sb.tile([P, PACK * S], BF16, name=f"{name}_woven", tag="woven", align_bytes=64)
            weave(woven[:], planes[:])
            codes = sb.tile([P, S], U32, name=f"{name}_codes", align_bytes=64)
            scales = sb.tile([P, S], U8, name=f"{name}_scales", align_bytes=64)
            nc.vector.quantize_mx(out=codes[:].bitcast(FP8X4), scales=scales[:], in_=woven[:])
            return codes, scales

        z2_w, z2_sc = quantise(z2_planes, "z2")
        b_bank = [ps.tile([P, S], F32, name=f"b_bank{t}", tag=f"B{t}") for t in range(PACK)]
        for t in range(PACK):
            product(b_bank[t], w3_d, w23_sd, W3_ROW, t, z2_w, z2_sc)
        z_w, z_sc = quantise(z_planes, "z")
        a_bank = [ps.tile([P, S], F32, name=f"a_bank{t}", tag=f"A{t}") for t in range(PACK)]
        for t in range(PACK):
            product(a_bank[t], w2_d, w23_sd, 0, t, z_w, z_sc)

        b_win = y_win
        tanh_b = sb.tile([P, PACK, S], F32, name="tanh_b")
        for t in range(PACK):
            nc.scalar.activation(tanh_b[:, t, :], b_bank[t][:], ACT.Tanh)
            nc.scalar.copy(b_win[t][:, :S], b_bank[t][:])
        for t in range(PACK):
            nc.scalar.copy(a_win[t][:, :S], a_bank[t][:])

        term_b = sb.tile([P, PACK, S], F32, name="term_b")
        result = sb.tile([P, PACK, S], F32, name="result")
        out_woven = sb.tile([P, PACK * S], BF16, name="out_woven", align_bytes=64)
        out_w = sb.tile([P, S], U32, name="out_w", align_bytes=64)
        out_sc = sb.tile([P, S], U8, name="out_sc", align_bytes=64)
        out_rows = out_0.rearrange("(p t) c -> p t c", t=PACK)
        out_words = out_1[0].rearrange("p c r -> p (c r)").bitcast(I32)
        for t in range(PACK):
            nc.vector.tensor_tensor(term_b[:, t, :], b_win[t][:].indirect(n5_t[:]), tanh_b[:, t, :], ALU.mult)

        pieces = [(t, 0, S) for t in range(PACK - 1)] + [(PACK - 1, 0, HALF), (PACK - 1, HALF, S)]
        for t, lo, hi in pieces:
            a_n4 = a_win[t][:].indirect(n4_t[:, lo // PER_COLUMN : hi // PER_COLUMN])
            nc.vector.tensor_tensor(result[:, t, lo:hi], a_n4, term_b[:, t, lo:hi], ALU.subtract)
            nc.sync.dma_start(out_rows[:, t, lo:hi], result[:, t, lo:hi])
        weave(out_woven[:, : PACK * HALF], result[:, :, :HALF], nc.scalar.copy)
        weave(out_woven[:, PACK * HALF :], result[:, :, HALF:])
        for lo in (0, HALF):
            cols = slice(lo, lo + HALF)
            nc.vector.quantize_mx(
                out=out_w[:, cols].bitcast(FP8X4), scales=out_sc[:, cols], in_=out_woven[:, PACK * lo : PACK * (lo + HALF)]
            )
            nc.sync.dma_start(out_words[:, cols], out_w[:, cols].bitcast(I32))
        for q in range(QUADRANTS):
            nc.scalar.dma_start(out_2[0, 4 * q : 4 * q + 4, :].bitcast(I32), out_sc[32 * q : 32 * q + 4, :].bitcast(I32))
